import numpy as np
import ml_dtypes


def mxq(x, axis, fmt="e4m3"):
    dtype, down = {"e4m3": (ml_dtypes.float8_e4m3fn, 7), "e5m2": (ml_dtypes.float8_e5m2, 14)}[fmt]
    v = np.moveaxis(np.asarray(x, np.float32).astype(ml_dtypes.bfloat16).astype(np.float64), axis, -1)
    blocks = v.reshape(v.shape[:-1] + (-1, 32))
    amax = np.abs(blocks).max(-1, keepdims=True)
    byte = np.maximum(np.where(amax > 0, np.frexp(amax)[1] - 1 + 127, 0) - down, 1)
    scale = np.exp2(byte - 127.0)
    codes = (blocks / scale).astype(np.float32).astype(dtype).astype(np.float64)
    return np.moveaxis((codes * scale).reshape(v.shape), -1, axis)


WIDE = False


def mx_kscale(k, group=512):
    if not WIDE:
        return np.ones(k)
    levels = np.array([18, -18])
    if group != 512:
        return np.exp2(np.random.permutation(np.resize(levels, k // group))).repeat(group)
    if k % 512:
        return np.exp2(np.random.permutation(np.resize(levels, k // 32))).repeat(32)
    a = np.empty((k // 512, 16))
    for p in range(k // 512):
        a[p, :8] = np.random.permutation(np.resize(levels, 8))
        for g in range(8):
            far = levels[np.abs(levels - a[p, g]) >= 10]
            a[p, g + 8] = far[np.random.randint(len(far))]
    return np.exp2(a.ravel()).repeat(32)


def f64(x):
    return np.asarray(x).astype(np.float64)


H, D, N = 4, 128, 512


def setup_inputs():
    n = np.random.standard_normal
    s = mx_kscale(D, 0)
    u = mx_kscale(N)
    t = np.random.uniform(0.5, 2.0, N) * u
    v = n((H, N, 128))
    return {
        "q": n((H, D, N)).astype(np.float32),
        "qa": (np.random.uniform(0.5, 2.0, D) * s)[:, None].astype(np.float32),
        "ka": np.tile(np.random.uniform(0.5, 2.0, D) / s, (128, 1)).astype(np.float32),
        "k": n((H, N, D)).astype(np.float32),
        "t": t.reshape(N, 1).astype(np.float32),
        "v": (v / t[:, None]).astype(np.float32),
    }


def reference(q, qa, ka, k, t, v):
    fq = (np.where(f64(q) > 0, f64(q) + 1.0, np.exp(np.minimum(f64(q), 0.0)))) * f64(qa)
    fk = (np.where(f64(k) > 0, f64(k) + 1.0, np.exp(np.minimum(f64(k), 0.0)))) * f64(t) * f64(ka)[:1]
    S = (mxq(fk, 1, "e4m3").transpose(0, 2, 1) @ mxq(f64(v), 1, "e4m3")) / N
    y = mxq(fq, 1, "e4m3").transpose(0, 2, 1) @ mxq(S, 1, "e4m3")
    return y

@@ -1,0 +1,274 @@
+from contextlib import ExitStack
+
+import concourse.mybir as mybir
+
+H, D, N, E = 4, 128, 512, 128
+FLOPS = 2 * H * N * D * E * 2
+BYTES = 4 * (2 * H * N * D + 2 * H * N * E + N + 2 * D)
+
+F32 = mybir.dt.float32
+BF16 = mybir.dt.bfloat16
+I32 = mybir.dt.int32
+U8 = mybir.dt.uint8
+FP8X4 = mybir.dt.float8_e4m3fn_x4
+ALU = mybir.AluOpType
+ACT = mybir.ActivationFunctionType
+
+P = 128
+PACK = 4
+ROWS = 32
+HALF = N // 2
+STRIDE = P + ROWS
+
+
+def tile_rows_lin_elu1_kernel(tc, q, qa, ka, k, t, v, out):
+    nc = tc.nc
+    with ExitStack() as ctx:
+        sb = ctx.enter_context(tc.tile_pool(name="sb", bufs=1))
+        ps = ctx.enter_context(tc.psum_pool(name="ps", bufs=1))
+        ctx.enter_context(tc.manual_schedule())
+
+        def f32(name, width):
+            return sb.tile([P, width], F32, name=name, align_bytes=64)
+
+        k_raw = [None] + [f32("k_raw%d" % h, 512) for h in range(1, H)]
+        k0_half = [f32("k0_half%d" % u, 256) for u in range(2)]
+        k_neg = [f32("k_neg%d" % h, 512) for h in range(H)]
+        k_exp = [f32("k_exp%d" % h, 512) for h in range(H)]
+        k_phi = [f32("k_phi%d" % h, 512) for h in range(H)]
+        v_raw = [f32("v_raw%d" % h, 512) for h in range(H)]
+        q_raw = [f32("q_raw%d" % u, 1024) for u in range(2)]
+        q_neg = [f32("q_neg%d" % c, 512) for c in range(4)]
+        q_exp = [f32("q_exp%d" % c, 512) for c in range(4)]
+        q_phi_a = f32("q_phi_a", 1024)
+        q_phi_b = [f32("q_phi_b%d" % c, 512) for c in range(2)]
+        t_sb = f32("t_sb", 8)
+        qa_sb = f32("qa_sb", 8)
+        ka_sb = f32("ka_sb", D)
+        tk = f32("tk", 512)
+        fk = sb.tile([P, 2048], BF16, name="fk", align_bytes=64)
+        vb = [sb.tile([P, 1024], BF16, name="vb%d" % a, align_bytes=64) for a in range(2)]
+        fq_a = sb.tile([P, 1024], BF16, name="fq_a", align_bytes=64)
+        fq_b = [sb.tile([P, 512], BF16, name="fq_b%d" % c, align_bytes=64) for c in range(2)]
+        s_bf = sb.tile([P, 512], BF16, name="s_bf", align_bytes=64)
+
+        def mx(name, words):
+            codes = sb.tile([P, words], I32, name=name + "_codes", align_bytes=64)
+            scales = sb.tile([P, words], U8, name=name + "_scales", align_bytes=64)
+            return codes, scales
+
+        k_mx = mx("k", 512)
+        v_mx = [mx("v%d" % a, 256) for a in range(2)]
+        qa_mx = mx("q_a", 256)
+        qb_mx = [mx("q_b%d" % c, 128) for c in range(2)]
+        s_mx = mx("s", 128)
+        k_wide = sb.tile([P, PACK, H * STRIDE], I32, name="k_wide", align_bytes=64)
+        y_a = [f32("y_a%d" % a, 512) for a in range(2)]
+        y_b = [f32("y_b%d" % c, 512) for c in range(2)]
+
+        s_bank = ps.tile([P, PACK, E], F32, name="s_bank")
+        y_bank = [ps.tile([P, 4, E], F32, name="y_bank%d" % h) for h in range(H)]
+        y_last = [y_bank[0]] + [ps.tile([P, 4, E], F32, name="y_last%d" % h) for h in range(1, H)]
+
+        def load_tokens(dst, src):
+            nc.sync.dma_start(out=dst[:], in_=src.rearrange("(p j) d -> p (j d)", j=PACK))
+
+        nc.scalar.dma_start(out=t_sb[:, 0:PACK], in_=t.rearrange("(p j) o -> p (j o)", j=PACK))
+        nc.scalar.dma_start(out=ka_sb[:], in_=ka)
+        k0_rows = k[0].rearrange("(p j) d -> p (j d)", j=PACK)
+        for u in range(2):
+            nc.sync.dma_start(out=k0_half[u][:], in_=k0_rows[:, u * 256 : (u + 1) * 256])
+        load_tokens(k_raw[1], k[1])
+        load_tokens(k_raw[2], k[2])
+        load_tokens(k_raw[3], k[3])
+        for h in range(H):
+            load_tokens(v_raw[h], v[h])
+        nc.sync.dma_start(
+            out=qa_sb[:, 0:PACK],
+            in_=qa.rearrange("(p j) o -> p (j o)", j=PACK).unsqueeze(0).to_broadcast([H, ROWS, PACK]),
+        )
+        q_rows = q.rearrange("h (p j) n -> (h p) j n", j=PACK)
+        for u in range(2):
+            nc.sync.dma_start(
+                out=q_raw[u][:].rearrange("p (j n) -> p j n", j=PACK),
+                in_=q_rows[:, :, u * HALF : (u + 1) * HALF],
+            )
+
+        def neg_v(dst, src):
+            nc.vector.tensor_scalar(out=dst, in0=src, scalar1=0.0, scalar2=None, op0=ALU.min)
+
+        def neg_s(dst, src):
+            nc.scalar.activation(out=dst, in_=src, func=ACT.Relu, scale=-1.0)
+
+        def exp_s(dst, src, sign):
+            nc.scalar.activation(out=dst, in_=src, func=ACT.Exp, scale=sign)
+
+        def phi(dst, raw, ex):
+            nc.vector.scalar_tensor_tensor(out=dst, in0=raw, scalar=1.0, in1=ex, op0=ALU.add, op1=ALU.max)
+
+        def quant(pair, src):
+            nc.vector.quantize_mx(out=pair[0][:].bitcast(FP8X4), scales=pair[1][:], in_=src[:])
+
+        def k_mul(h):
+            nc.vector.tensor_tensor(
+                out=fk[:].rearrange("p (x h a j) -> p h a j x", x=PACK, h=H, j=PACK)[:, h],
+                in0=k_phi[h][:].rearrange("p (j a x) -> p a j x", j=PACK, x=PACK),
+                in1=tk[:].rearrange("p (a j x) -> p a j x", j=PACK, x=PACK),
+                op=ALU.mult,
+            )
+
+        def v_round(h):
+            nc.scalar.copy(
+                out=vb[h // 2][:, (h % 2) * 512 : (h % 2 + 1) * 512].rearrange("p (c i j) -> p c j i", i=2, j=PACK),
+                in_=v_raw[h][:].rearrange("p (j c i) -> p c j i", j=PACK, i=2),
+            )
+
+        def jn(ap):
+            return ap.rearrange("p (j n) -> p j n", j=PACK)
+
+        q_src = [
+            q_raw[0][:, 0:512],
+            q_raw[0][:, 512:1024],
+            jn(q_raw[1][:])[:, :, 0:128],
+            jn(q_raw[1][:])[:, :, 128:256],
+        ]
+        q_view = [lambda ap: ap, lambda ap: ap, jn, jn]
+        q_dst = [q_phi_a[:, 0:512], q_phi_a[:, 512:1024], jn(q_phi_b[0][:]), jn(q_phi_b[1][:])]
+
+        def q_neg_s(c):
+            neg_s(q_view[c](q_neg[c][:]), q_src[c])
+
+        def q_exp_s(c):
+            exp_s(q_exp[c][:], q_neg[c][:], -1.0)
+
+        def q_phi(c):
+            phi(q_dst[c], q_src[c], q_view[c](q_exp[c][:]))
+
+        def q_mul_a():
+            nc.vector.tensor_tensor(
+                out=fq_a[:].rearrange("p (r s j) -> p s j r", r=2, j=PACK),
+                in0=q_phi_a[:].rearrange("p (j s r) -> p s j r", j=PACK, r=2),
+                in1=qa_sb[:, 0:PACK].unsqueeze(1).unsqueeze(3).to_broadcast([P, 128, PACK, 2]),
+                op=ALU.mult,
+            )
+
+        def q_mul_b(c):
+            nc.vector.tensor_tensor(
+                out=fq_b[c][:].rearrange("p (c i j) -> p c j i", i=2, j=PACK),
+                in0=q_phi_b[c][:].rearrange("p (j c i) -> p c j i", j=PACK, i=2),
+                in1=qa_sb[:, 0:PACK].unsqueeze(1).unsqueeze(3).to_broadcast([P, 64, PACK, 2]),
+                op=ALU.mult,
+            )
+
+        def read_state(bank_ap, h, pair, cols):
+            rows = slice(ROWS * h, ROWS * (h + 1))
+            nc.tensor.matmul_mx(
+                out=bank_ap,
+                lhsT=pair[0][rows, cols].bitcast(FP8X4),
+                lhsT_scale=pair[1][rows, cols],
+                rhs=s_mx[0][rows, :].bitcast(FP8X4),
+                rhs_scale=s_mx[1][rows, :],
+                start=True,
+                stop=True,
+            )
+
+        nc.vector.memset(k_wide[:, :, 0 : H * P], 0)
+        nc.vector.tensor_tensor(
+            out=tk[:].rearrange("p (a j x) -> p a j x", j=PACK, x=PACK),
+            in0=ka_sb[:].rearrange("p (a x) -> p a x", x=PACK).unsqueeze(2).to_broadcast([P, ROWS, PACK, PACK]),
+            in1=t_sb[:, 0:PACK].unsqueeze(1).unsqueeze(3).to_broadcast([P, ROWS, PACK, PACK]),
+            op=ALU.mult,
+        )
+        for u in range(2):
+            half = slice(u * 256, (u + 1) * 256)
+            neg_v(k_neg[0][:, half], k0_half[u][:])
+            exp_s(k_exp[0][:, half], k_neg[0][:, half], 1.0)
+        neg_v(k_neg[1][:], k_raw[1][:])
+        exp_s(k_exp[1][:], k_neg[1][:], 1.0)
+        for h in (2, 3):
+            neg_s(k_neg[h][:], k_raw[h][:])
+        for h in (2, 3):
+            exp_s(k_exp[h][:], k_neg[h][:], -1.0)
+        for u in range(2):
+            half = slice(u * 256, (u + 1) * 256)
+            phi(k_phi[0][:, half], k0_half[u][:], k_exp[0][:, half])
+        k_mul(0)
+        phi(k_phi[1][:], k_raw[1][:], k_exp[1][:])
+        phi(k_phi[2][:], k_raw[2][:], k_exp[2][:])
+        k_mul(1)
+        phi(k_phi[3][:], k_raw[3][:], k_exp[3][:])
+        k_mul(2)
+        k_mul(3)
+        for h in range(H):
+            v_round(h)
+        neg_v(q_neg[0][:], q_src[0])
+        quant(k_mx, fk)
+        quant(v_mx[0], vb[0])
+        nc.vector.tensor_copy(
+            out=k_wide[:].rearrange("p x (h c) -> p x h c", c=STRIDE)[:, :, :, 0:ROWS],
+            in_=k_mx[0][:].rearrange("p (x h c) -> p x h c", x=PACK, h=H),
+        )
+        quant(v_mx[1], vb[1])
+        for x in range(PACK):
+            for h in range(H):
+                cols = slice((h % 2) * E, (h % 2 + 1) * E)
+                nc.tensor.matmul_mx(
+                    out=s_bank[:, x, :],
+                    lhsT=k_wide[:, x, P * h : P * (h + 1)].bitcast(FP8X4),
+                    lhsT_scale=k_mx[1][:, P * x : P * (x + 1)],
+                    rhs=v_mx[h // 2][0][:, cols].bitcast(FP8X4),
+                    rhs_scale=v_mx[h // 2][1][:, cols],
+                    start=(h == 0),
+                    stop=(h == H - 1),
+                )
+
+        exp_s(q_exp[0][:], q_neg[0][:], 1.0)
+        q_neg_s(1)
+        q_neg_s(2)
+        q_exp_s(1)
+        q_neg_s(3)
+        q_exp_s(2)
+        q_exp_s(3)
+        nc.scalar.activation(
+            out=s_bf[:].rearrange("p (e x) -> p e x", x=PACK),
+            in_=s_bank[:].rearrange("p x e -> p e x"),
+            func=ACT.Copy,
+            scale=1.0 / N,
+        )
+        q_phi(0)
+        q_phi(1)
+        q_phi(2)
+        q_mul_a()
+        q_phi(3)
+        quant(s_mx, s_bf)
+        quant(qa_mx, fq_a)
+        for r in range(2):
+            for h in range(H):
+                read_state(y_bank[h][:, r, :], h, qa_mx, slice(r * P, (r + 1) * P))
+        out_a = out[:, 0:HALF, :].rearrange("h (s r) e -> s h (r e)", r=2)
+        for a in range(2):
+            for h in (2 * a, 2 * a + 1):
+                nc.scalar.copy(
+                    out=y_a[a][:, (h % 2) * 256 : (h % 2 + 1) * 256],
+                    in_=y_bank[h][:, 0:2, :].rearrange("p r e -> p (r e)"),
+                )
+            nc.sync.dma_start(out=out_a[:, 2 * a : 2 * a + 2, :], in_=y_a[a][:].rearrange("p (h w) -> p h w", h=2))
+        q_mul_b(0)
+        q_mul_b(1)
+        quant(qb_mx[0], fq_b[0])
+        quant(qb_mx[1], fq_b[1])
+        for c in range(2):
+            banks = y_bank if c == 0 else y_last
+            for h in range(H):
+                read_state(banks[h][:, 2 + c, :], h, qb_mx[c], slice(0, P))
+            for h in range(H):
+                dst = y_b[c][:, h * E : (h + 1) * E]
+                if c == 1 and h >= 2:
+                    nc.vector.tensor_copy(out=dst, in_=banks[h][:, 2 + c, :])
+                else:
+                    nc.scalar.copy(out=dst, in_=banks[h][:, 2 + c, :])
+            n0 = HALF + c * P
+            nc.sync.dma_start(
+                out=out[:, n0 : n0 + P, :].rearrange("h s e -> s h e"),
+                in_=y_b[c][:].rearrange("p (h e) -> p h e", h=H),
+            )

@@ -46,7 +46,7 @@ def tile_rows_lin_elu1_kernel(tc, q, qa, ka, k, t, v, out):
         qa_sb = f32("qa_sb", 8)
         ka_sb = f32("ka_sb", D)
         tk = f32("tk", 512)
-        fk = sb.tile([P, 2048], BF16, name="fk", align_bytes=64)
+        fk = [sb.tile([P, 1024], BF16, name="fk%d" % a, align_bytes=64) for a in range(2)]
         vb = [sb.tile([P, 1024], BF16, name="vb%d" % a, align_bytes=64) for a in range(2)]
         fq_a = sb.tile([P, 1024], BF16, name="fq_a", align_bytes=64)
         fq_b = [sb.tile([P, 512], BF16, name="fq_b%d" % c, align_bytes=64) for c in range(2)]
@@ -57,18 +57,19 @@ def tile_rows_lin_elu1_kernel(tc, q, qa, ka, k, t, v, out):
             scales = sb.tile([P, words], U8, name=name + "_scales", align_bytes=64)
             return codes, scales
 
-        k_mx = mx("k", 512)
+        k_codes = [sb.tile([P, 256], I32, name="k_codes%d" % a, align_bytes=64) for a in range(2)]
+        k_scales = sb.tile([P, 768], U8, name="k_scales", align_bytes=64)
         v_mx = [mx("v%d" % a, 256) for a in range(2)]
         qa_mx = mx("q_a", 256)
         qb_mx = [mx("q_b%d" % c, 128) for c in range(2)]
         s_mx = mx("s", 128)
-        k_wide = sb.tile([P, PACK, H * STRIDE], I32, name="k_wide", align_bytes=64)
+        k_wide = [sb.tile([P, PACK, 384], I32, name="k_wide%d" % a, align_bytes=64) for a in range(2)]
         y_a = [f32("y_a%d" % a, 512) for a in range(2)]
         y_b = [f32("y_b%d" % c, 512) for c in range(2)]
 
-        s_bank = ps.tile([P, PACK, E], F32, name="s_bank")
+        s_bank = [ps.tile([P, PACK, E], F32, name="s_bank%d" % a) for a in range(2)]
         y_bank = [ps.tile([P, 4, E], F32, name="y_bank%d" % h) for h in range(H)]
-        y_last = [y_bank[0]] + [ps.tile([P, 4, E], F32, name="y_last%d" % h) for h in range(1, H)]
+        y_mid = y_bank[0:2] + [ps.tile([P, 4, E], F32, name="y_mid%d" % h) for h in range(2, H)]
 
         def load_tokens(dst, src):
             nc.sync.dma_start(out=dst[:], in_=src.rearrange("(p j) d -> p (j d)", j=PACK))
@@ -83,10 +84,10 @@ def tile_rows_lin_elu1_kernel(tc, q, qa, ka, k, t, v, out):
         load_tokens(k_raw[3], k[3])
         for h in range(H):
             load_tokens(v_raw[h], v[h])
-        nc.sync.dma_start(
-            out=qa_sb[:, 0:PACK],
-            in_=qa.rearrange("(p j) o -> p (j o)", j=PACK).unsqueeze(0).to_broadcast([H, ROWS, PACK]),
-        )
+        for h in range(H):
+            nc.sync.dma_start(
+                out=qa_sb[ROWS * h : ROWS * (h + 1), 0:PACK], in_=qa.rearrange("(p j) o -> p (j o)", j=PACK)
+            )
         q_rows = q.rearrange("h (p j) n -> (h p) j n", j=PACK)
         for u in range(2):
             nc.sync.dma_start(
@@ -111,9 +112,9 @@ def tile_rows_lin_elu1_kernel(tc, q, qa, ka, k, t, v, out):
 
         def k_mul(h):
             nc.vector.tensor_tensor(
-                out=fk[:].rearrange("p (x h a j) -> p h a j x", x=PACK, h=H, j=PACK)[:, h],
+                out=fk[h // 2][:].rearrange("p (x g a j) -> p g a j x", x=PACK, g=2, j=PACK)[:, h % 2],
                 in0=k_phi[h][:].rearrange("p (j a x) -> p a j x", j=PACK, x=PACK),
-                in1=tk[:].rearrange("p (a j x) -> p a j x", j=PACK, x=PACK),
+                in1=tk[:].rearrange("p (j a x) -> p a j x", j=PACK, x=PACK),
                 op=ALU.mult,
             )
 
@@ -172,74 +173,95 @@ def tile_rows_lin_elu1_kernel(tc, q, qa, ka, k, t, v, out):
                 stop=True,
             )
 
-        nc.vector.memset(k_wide[:, :, 0 : H * P], 0)
-        nc.vector.tensor_tensor(
-            out=tk[:].rearrange("p (a j x) -> p a j x", j=PACK, x=PACK),
-            in0=ka_sb[:].rearrange("p (a x) -> p a x", x=PACK).unsqueeze(2).to_broadcast([P, ROWS, PACK, PACK]),
-            in1=t_sb[:, 0:PACK].unsqueeze(1).unsqueeze(3).to_broadcast([P, ROWS, PACK, PACK]),
-            op=ALU.mult,
-        )
+        def k_quant(a):
+            nc.vector.quantize_mx(
+                out=k_codes[a][:].bitcast(FP8X4), scales=k_scales[:, 384 * a + 64 : 384 * a + 320], in_=fk[a][:]
+            )
+
+        def k_spread(a):
+            live = k_wide[a][:, :, 64 * a : 64 * a + 2 * STRIDE].rearrange("p x (g c) -> p x g c", c=STRIDE)
+            nc.vector.tensor_copy(
+                out=live[:, :, :, 0:ROWS],
+                in_=k_codes[a][:].rearrange("p (x g c) -> p x g c", x=PACK, g=2),
+            )
+
+        def build_state(a):
+            for x in range(PACK):
+                first = 384 * a + 64 * x + 64 * (1 - a)
+                for g in range(2):
+                    cols = slice(g * E, (g + 1) * E)
+                    nc.tensor.matmul_mx(
+                        out=s_bank[a][:, x, :],
+                        lhsT=k_wide[a][:, x, P * g : P * (g + 1)].bitcast(FP8X4),
+                        lhsT_scale=k_scales[:, first : first + P],
+                        rhs=v_mx[a][0][:, cols].bitcast(FP8X4),
+                        rhs_scale=v_mx[a][1][:, cols],
+                        start=(g == 0),
+                        stop=(g == 1),
+                    )
+
+        def state_out(a):
+            rows = slice(64 * a, 64 * (a + 1))
+            nc.scalar.activation(
+                out=s_bf[rows, :].rearrange("p (e x) -> p e x", x=PACK),
+                in_=s_bank[a][rows].rearrange("p x e -> p e x"),
+                func=ACT.Copy,
+                scale=1.0 / N,
+            )
+
+        nc.vector.memset(k_scales[:].bitcast(I32), 0)
+        for a in range(2):
+            nc.vector.memset(k_wide[a][:, :, 0 : 2 * P], 0)
         for u in range(2):
             half = slice(u * 256, (u + 1) * 256)
             neg_v(k_neg[0][:, half], k0_half[u][:])
             exp_s(k_exp[0][:, half], k_neg[0][:, half], 1.0)
+        for j in range(PACK):
+            nc.vector.tensor_scalar(
+                out=tk[:, j * D : (j + 1) * D], in0=ka_sb[:], scalar1=t_sb[:, j : j + 1], scalar2=None, op0=ALU.mult
+            )
         neg_v(k_neg[1][:], k_raw[1][:])
         exp_s(k_exp[1][:], k_neg[1][:], 1.0)
-        for h in (2, 3):
-            neg_s(k_neg[h][:], k_raw[h][:])
-        for h in (2, 3):
-            exp_s(k_exp[h][:], k_neg[h][:], -1.0)
         for u in range(2):
             half = slice(u * 256, (u + 1) * 256)
             phi(k_phi[0][:, half], k0_half[u][:], k_exp[0][:, half])
+        neg_v(k_neg[2][:], k_raw[2][:])
+        exp_s(k_exp[2][:], k_neg[2][:], 1.0)
+        neg_s(k_neg[3][:], k_raw[3][:])
+        v_round(0)
+        exp_s(k_exp[3][:], k_neg[3][:], -1.0)
+        for h in range(1, H):
+            v_round(h)
         k_mul(0)
         phi(k_phi[1][:], k_raw[1][:], k_exp[1][:])
         phi(k_phi[2][:], k_raw[2][:], k_exp[2][:])
         k_mul(1)
-        phi(k_phi[3][:], k_raw[3][:], k_exp[3][:])
         k_mul(2)
-        k_mul(3)
-        for h in range(H):
-            v_round(h)
-        neg_v(q_neg[0][:], q_src[0])
-        quant(k_mx, fk)
+        k_quant(0)
+        phi(k_phi[3][:], k_raw[3][:], k_exp[3][:])
+        k_spread(0)
         quant(v_mx[0], vb[0])
-        nc.vector.tensor_copy(
-            out=k_wide[:].rearrange("p x (h c) -> p x h c", c=STRIDE)[:, :, :, 0:ROWS],
-            in_=k_mx[0][:].rearrange("p (x h c) -> p x h c", x=PACK, h=H),
-        )
+        k_mul(3)
+        build_state(0)
+        neg_v(q_neg[1][:], q_src[1])
+        k_quant(1)
         quant(v_mx[1], vb[1])
-        for x in range(PACK):
-            for h in range(H):
-                cols = slice((h % 2) * E, (h % 2 + 1) * E)
-                nc.tensor.matmul_mx(
-                    out=s_bank[:, x, :],
-                    lhsT=k_wide[:, x, P * h : P * (h + 1)].bitcast(FP8X4),
-                    lhsT_scale=k_mx[1][:, P * x : P * (x + 1)],
-                    rhs=v_mx[h // 2][0][:, cols].bitcast(FP8X4),
-                    rhs_scale=v_mx[h // 2][1][:, cols],
-                    start=(h == 0),
-                    stop=(h == H - 1),
-                )
+        k_spread(1)
+        build_state(1)
 
-        exp_s(q_exp[0][:], q_neg[0][:], 1.0)
-        q_neg_s(1)
+        q_neg_s(0)
+        q_exp_s(0)
+        exp_s(q_exp[1][:], q_neg[1][:], 1.0)
         q_neg_s(2)
-        q_exp_s(1)
-        q_neg_s(3)
+        state_out(0)
         q_exp_s(2)
+        state_out(1)
+        q_neg_s(3)
         q_exp_s(3)
-        nc.scalar.activation(
-            out=s_bf[:].rearrange("p (e x) -> p e x", x=PACK),
-            in_=s_bank[:].rearrange("p x e -> p e x"),
-            func=ACT.Copy,
-            scale=1.0 / N,
-        )
         q_phi(0)
         q_phi(1)
-        q_phi(2)
         q_mul_a()
-        q_phi(3)
+        q_phi(2)
         quant(s_mx, s_bf)
         quant(qa_mx, fq_a)
         for r in range(2):
@@ -254,11 +276,12 @@ def tile_rows_lin_elu1_kernel(tc, q, qa, ka, k, t, v, out):
                 )
             nc.sync.dma_start(out=out_a[:, 2 * a : 2 * a + 2, :], in_=y_a[a][:].rearrange("p (h w) -> p h w", h=2))
         q_mul_b(0)
-        q_mul_b(1)
+        q_phi(3)
         quant(qb_mx[0], fq_b[0])
+        q_mul_b(1)
         quant(qb_mx[1], fq_b[1])
         for c in range(2):
-            banks = y_bank if c == 0 else y_last
+            banks = y_mid if c == 0 else y_bank
             for h in range(H):
                 read_state(banks[h][:, 2 + c, :], h, qb_mx[c], slice(0, P))
             for h in range(H):
@@ -268,7 +291,10 @@ def tile_rows_lin_elu1_kernel(tc, q, qa, ka, k, t, v, out):
                 else:
                     nc.scalar.copy(out=dst, in_=banks[h][:, 2 + c, :])
             n0 = HALF + c * P
-            nc.sync.dma_start(
-                out=out[:, n0 : n0 + P, :].rearrange("h s e -> s h e"),
-                in_=y_b[c][:].rearrange("p (h e) -> p h e", h=H),
-            )
+            out_b = out[:, n0 : n0 + P, :].rearrange("h s e -> s h e")
+            y_view = y_b[c][:].rearrange("p (h e) -> p h e", h=H)
+            if c == 0:
+                nc.sync.dma_start(out=out_b, in_=y_view)
+            else:
+                nc.scalar.dma_start(out=out_b[:, 0:2, :], in_=y_view[:, 0:2, :])
+                nc.sync.dma_start(out=out_b[:, 2:4, :], in_=y_view[:, 2:4, :])

@@ -40,8 +40,7 @@ def tile_rows_lin_elu1_kernel(tc, q, qa, ka, k, t, v, out):
         q_raw = [f32("q_raw%d" % u, 1024) for u in range(2)]
         q_neg = [f32("q_neg%d" % c, 512) for c in range(4)]
         q_exp = [f32("q_exp%d" % c, 512) for c in range(4)]
-        q_phi_a = f32("q_phi_a", 1024)
-        q_phi_b = [f32("q_phi_b%d" % c, 512) for c in range(2)]
+        q_map = [f32("q_map%d" % c, 512) for c in range(4)]
         t_sb = f32("t_sb", 8)
         qa_sb = f32("qa_sb", 8)
         ka_sb = f32("ka_sb", D)
@@ -64,12 +63,12 @@ def tile_rows_lin_elu1_kernel(tc, q, qa, ka, k, t, v, out):
         qb_mx = [mx("q_b%d" % c, 128) for c in range(2)]
         s_mx = mx("s", 128)
         k_wide = [sb.tile([P, PACK, 384], I32, name="k_wide%d" % a, align_bytes=64) for a in range(2)]
-        y_a = [f32("y_a%d" % a, 512) for a in range(2)]
+        y_a = [f32("y_a%d" % h, 256) for h in range(H)]
         y_b = [f32("y_b%d" % c, 512) for c in range(2)]
 
-        s_bank = [ps.tile([P, PACK, E], F32, name="s_bank%d" % a) for a in range(2)]
+        s_bank = ps.tile([P, PACK, E], F32, name="s_bank")
         y_bank = [ps.tile([P, 4, E], F32, name="y_bank%d" % h) for h in range(H)]
-        y_mid = y_bank[0:2] + [ps.tile([P, 4, E], F32, name="y_mid%d" % h) for h in range(2, H)]
+        y_mid = y_bank[0:1] + [ps.tile([P, 4, E], F32, name="y_mid%d" % h) for h in range(1, H)]
 
         def load_tokens(dst, src):
             nc.sync.dma_start(out=dst[:], in_=src.rearrange("(p j) d -> p (j d)", j=PACK))
@@ -127,36 +126,29 @@ def tile_rows_lin_elu1_kernel(tc, q, qa, ka, k, t, v, out):
         def jn(ap):
             return ap.rearrange("p (j n) -> p j n", j=PACK)
 
-        q_src = [
-            q_raw[0][:, 0:512],
-            q_raw[0][:, 512:1024],
-            jn(q_raw[1][:])[:, :, 0:128],
-            jn(q_raw[1][:])[:, :, 128:256],
-        ]
-        q_view = [lambda ap: ap, lambda ap: ap, jn, jn]
-        q_dst = [q_phi_a[:, 0:512], q_phi_a[:, 512:1024], jn(q_phi_b[0][:]), jn(q_phi_b[1][:])]
+        q_src = [jn(q_raw[c // 2][:])[:, :, (c % 2) * P : (c % 2 + 1) * P] for c in range(4)]
 
         def q_neg_s(c):
-            neg_s(q_view[c](q_neg[c][:]), q_src[c])
+            neg_s(jn(q_neg[c][:]), q_src[c])
 
         def q_exp_s(c):
             exp_s(q_exp[c][:], q_neg[c][:], -1.0)
 
         def q_phi(c):
-            phi(q_dst[c], q_src[c], q_view[c](q_exp[c][:]))
+            phi(jn(q_map[c][:]), q_src[c], jn(q_exp[c][:]))
 
-        def q_mul_a():
+        def q_mul_a(c):
             nc.vector.tensor_tensor(
-                out=fq_a[:].rearrange("p (r s j) -> p s j r", r=2, j=PACK),
-                in0=q_phi_a[:].rearrange("p (j s r) -> p s j r", j=PACK, r=2),
-                in1=qa_sb[:, 0:PACK].unsqueeze(1).unsqueeze(3).to_broadcast([P, 128, PACK, 2]),
+                out=fq_a[:].rearrange("p (r s j) -> p s j r", r=2, j=PACK)[:, 64 * c : 64 * (c + 1)],
+                in0=q_map[c][:].rearrange("p (j s r) -> p s j r", j=PACK, r=2),
+                in1=qa_sb[:, 0:PACK].unsqueeze(1).unsqueeze(3).to_broadcast([P, 64, PACK, 2]),
                 op=ALU.mult,
             )
 
         def q_mul_b(c):
             nc.vector.tensor_tensor(
                 out=fq_b[c][:].rearrange("p (c i j) -> p c j i", i=2, j=PACK),
-                in0=q_phi_b[c][:].rearrange("p (j c i) -> p c j i", j=PACK, i=2),
+                in0=q_map[2 + c][:].rearrange("p (j c i) -> p c j i", j=PACK, i=2),
                 in1=qa_sb[:, 0:PACK].unsqueeze(1).unsqueeze(3).to_broadcast([P, 64, PACK, 2]),
                 op=ALU.mult,
             )
@@ -191,20 +183,19 @@ def tile_rows_lin_elu1_kernel(tc, q, qa, ka, k, t, v, out):
                 for g in range(2):
                     cols = slice(g * E, (g + 1) * E)
                     nc.tensor.matmul_mx(
-                        out=s_bank[a][:, x, :],
+                        out=s_bank[:, x, :],
                         lhsT=k_wide[a][:, x, P * g : P * (g + 1)].bitcast(FP8X4),
                         lhsT_scale=k_scales[:, first : first + P],
                         rhs=v_mx[a][0][:, cols].bitcast(FP8X4),
                         rhs_scale=v_mx[a][1][:, cols],
-                        start=(g == 0),
-                        stop=(g == 1),
+                        start=(a == 0 and x == 0 and g == 0),
+                        stop=(a == 1 and x == PACK - 1 and g == 1),
                     )
 
-        def state_out(a):
-            rows = slice(64 * a, 64 * (a + 1))
+        def state_out():
             nc.scalar.activation(
-                out=s_bf[rows, :].rearrange("p (e x) -> p e x", x=PACK),
-                in_=s_bank[a][rows].rearrange("p x e -> p e x"),
+                out=s_bf[:].rearrange("p (e x) -> p e x", x=PACK),
+                in_=s_bank[:].rearrange("p x e -> p e x"),
                 func=ACT.Copy,
                 scale=1.0 / N,
             )
@@ -243,7 +234,7 @@ def tile_rows_lin_elu1_kernel(tc, q, qa, ka, k, t, v, out):
         quant(v_mx[0], vb[0])
         k_mul(3)
         build_state(0)
-        neg_v(q_neg[1][:], q_src[1])
+        neg_v(jn(q_neg[1][:]), q_src[1])
         k_quant(1)
         quant(v_mx[1], vb[1])
         k_spread(1)
@@ -253,28 +244,24 @@ def tile_rows_lin_elu1_kernel(tc, q, qa, ka, k, t, v, out):
         q_exp_s(0)
         exp_s(q_exp[1][:], q_neg[1][:], 1.0)
         q_neg_s(2)
-        state_out(0)
-        q_exp_s(2)
-        state_out(1)
         q_neg_s(3)
+        q_exp_s(2)
+        state_out()
         q_exp_s(3)
         q_phi(0)
         q_phi(1)
-        q_mul_a()
+        q_mul_a(0)
+        q_mul_a(1)
         q_phi(2)
         quant(s_mx, s_bf)
         quant(qa_mx, fq_a)
-        for r in range(2):
-            for h in range(H):
+        for h in range(H):
+            for r in range(2):
                 read_state(y_bank[h][:, r, :], h, qa_mx, slice(r * P, (r + 1) * P))
         out_a = out[:, 0:HALF, :].rearrange("h (s r) e -> s h (r e)", r=2)
-        for a in range(2):
-            for h in (2 * a, 2 * a + 1):
-                nc.scalar.copy(
-                    out=y_a[a][:, (h % 2) * 256 : (h % 2 + 1) * 256],
-                    in_=y_bank[h][:, 0:2, :].rearrange("p r e -> p (r e)"),
-                )
-            nc.sync.dma_start(out=out_a[:, 2 * a : 2 * a + 2, :], in_=y_a[a][:].rearrange("p (h w) -> p h w", h=2))
+        for h in range(H):
+            nc.scalar.copy(out=y_a[h][:], in_=y_bank[h][:, 0:2, :].rearrange("p r e -> p (r e)"))
+            nc.sync.dma_start(out=out_a[:, h, :], in_=y_a[h][:])
         q_mul_b(0)
         q_phi(3)
         quant(qb_mx[0], fq_b[0])
@@ -284,17 +271,14 @@ def tile_rows_lin_elu1_kernel(tc, q, qa, ka, k, t, v, out):
             banks = y_mid if c == 0 else y_bank
             for h in range(H):
                 read_state(banks[h][:, 2 + c, :], h, qb_mx[c], slice(0, P))
-            for h in range(H):
-                dst = y_b[c][:, h * E : (h + 1) * E]
-                if c == 1 and h >= 2:
-                    nc.vector.tensor_copy(out=dst, in_=banks[h][:, 2 + c, :])
-                else:
-                    nc.scalar.copy(out=dst, in_=banks[h][:, 2 + c, :])
             n0 = HALF + c * P
             out_b = out[:, n0 : n0 + P, :].rearrange("h s e -> s h e")
             y_view = y_b[c][:].rearrange("p (h e) -> p h e", h=H)
-            if c == 0:
-                nc.sync.dma_start(out=out_b, in_=y_view)
-            else:
-                nc.scalar.dma_start(out=out_b[:, 0:2, :], in_=y_view[:, 0:2, :])
-                nc.sync.dma_start(out=out_b[:, 2:4, :], in_=y_view[:, 2:4, :])
+            for a in range(2):
+                for h in (2 * a, 2 * a + 1):
+                    if c == 1 and a == 1:
+                        nc.vector.tensor_copy(out=y_view[:, h, :], in_=banks[h][:, 2 + c, :])
+                    else:
+                        nc.scalar.copy(out=y_view[:, h, :], in_=banks[h][:, 2 + c, :])
+                queue = nc.scalar if (c == 1 and a == 0) else nc.sync
+                queue.dma_start(out=out_b[:, 2 * a : 2 * a + 2, :], in_=y_view[:, 2 * a : 2 * a + 2, :])

from contextlib import ExitStack

import concourse.mybir as mybir

H, D, N, E = 4, 128, 512, 128
FLOPS = 2 * H * N * D * E * 2
BYTES = 4 * (2 * H * N * D + 2 * H * N * E + N + 2 * D)

F32 = mybir.dt.float32
BF16 = mybir.dt.bfloat16
I32 = mybir.dt.int32
U8 = mybir.dt.uint8
FP8X4 = mybir.dt.float8_e4m3fn_x4
ALU = mybir.AluOpType
ACT = mybir.ActivationFunctionType

P = 128
PACK = 4
ROWS = 32
HALF = N // 2
STRIDE = P + ROWS


def tile_rows_lin_elu1_kernel(tc, q, qa, ka, k, t, v, out):
    nc = tc.nc
    with ExitStack() as ctx:
        sb = ctx.enter_context(tc.tile_pool(name="sb", bufs=1))
        ps = ctx.enter_context(tc.psum_pool(name="ps", bufs=1))
        ctx.enter_context(tc.manual_schedule())

        def f32(name, width):
            return sb.tile([P, width], F32, name=name, align_bytes=64)

        k_raw = [None] + [f32("k_raw%d" % h, 512) for h in range(1, H)]
        k0_half = [f32("k0_half%d" % u, 256) for u in range(2)]
        k_neg = [f32("k_neg%d" % h, 512) for h in range(H)]
        k_exp = [f32("k_exp%d" % h, 512) for h in range(H)]
        k_phi = [f32("k_phi%d" % h, 512) for h in range(H)]
        v_raw = [f32("v_raw%d" % h, 512) for h in range(H)]
        q_raw = [f32("q_raw%d" % u, 1024) for u in range(2)]
        q_neg = [f32("q_neg%d" % c, 512) for c in range(4)]
        q_exp = [f32("q_exp%d" % c, 512) for c in range(4)]
        q_map = [f32("q_map%d" % c, 512) for c in range(4)]
        t_sb = f32("t_sb", 8)
        qa_sb = f32("qa_sb", 8)
        ka_sb = f32("ka_sb", D)
        tk = f32("tk", 512)
        fk = [sb.tile([P, 1024], BF16, name="fk%d" % a, align_bytes=64) for a in range(2)]
        vb = [sb.tile([P, 1024], BF16, name="vb%d" % a, align_bytes=64) for a in range(2)]
        fq_a = sb.tile([P, 1024], BF16, name="fq_a", align_bytes=64)
        fq_b = [sb.tile([P, 512], BF16, name="fq_b%d" % c, align_bytes=64) for c in range(2)]
        s_bf = sb.tile([P, 512], BF16, name="s_bf", align_bytes=64)

        def mx(name, words):
            codes = sb.tile([P, words], I32, name=name + "_codes", align_bytes=64)
            scales = sb.tile([P, words], U8, name=name + "_scales", align_bytes=64)
            return codes, scales

        k_codes = [sb.tile([P, 256], I32, name="k_codes%d" % a, align_bytes=64) for a in range(2)]
        k_scales = sb.tile([P, 768], U8, name="k_scales", align_bytes=64)
        v_mx = [mx("v%d" % a, 256) for a in range(2)]
        qa_mx = mx("q_a", 256)
        qb_mx = [mx("q_b%d" % c, 128) for c in range(2)]
        s_mx = mx("s", 128)
        k_wide = [sb.tile([P, PACK, 384], I32, name="k_wide%d" % a, align_bytes=64) for a in range(2)]
        y_a = [f32("y_a%d" % h, 256) for h in range(H)]
        y_b = [f32("y_b%d" % c, 512) for c in range(2)]

        s_bank = ps.tile([P, PACK, E], F32, name="s_bank")
        y_bank = [ps.tile([P, 4, E], F32, name="y_bank%d" % h) for h in range(H)]
        y_mid = y_bank[0:1] + [ps.tile([P, 4, E], F32, name="y_mid%d" % h) for h in range(1, H)]

        def load_tokens(dst, src):
            nc.sync.dma_start(out=dst[:], in_=src.rearrange("(p j) d -> p (j d)", j=PACK))

        nc.scalar.dma_start(out=t_sb[:, 0:PACK], in_=t.rearrange("(p j) o -> p (j o)", j=PACK))
        nc.scalar.dma_start(out=ka_sb[:], in_=ka)
        k0_rows = k[0].rearrange("(p j) d -> p (j d)", j=PACK)
        for u in range(2):
            nc.sync.dma_start(out=k0_half[u][:], in_=k0_rows[:, u * 256 : (u + 1) * 256])
        load_tokens(k_raw[1], k[1])
        load_tokens(k_raw[2], k[2])
        load_tokens(k_raw[3], k[3])
        for h in range(H):
            load_tokens(v_raw[h], v[h])
        for h in range(H):
            nc.sync.dma_start(
                out=qa_sb[ROWS * h : ROWS * (h + 1), 0:PACK], in_=qa.rearrange("(p j) o -> p (j o)", j=PACK)
            )
        q_rows = q.rearrange("h (p j) n -> (h p) j n", j=PACK)
        for u in range(2):
            nc.sync.dma_start(
                out=q_raw[u][:].rearrange("p (j n) -> p j n", j=PACK),
                in_=q_rows[:, :, u * HALF : (u + 1) * HALF],
            )

        def neg_v(dst, src):
            nc.vector.tensor_scalar(out=dst, in0=src, scalar1=0.0, scalar2=None, op0=ALU.min)

        def neg_s(dst, src):
            nc.scalar.activation(out=dst, in_=src, func=ACT.Relu, scale=-1.0)

        def exp_s(dst, src, sign):
            nc.scalar.activation(out=dst, in_=src, func=ACT.Exp, scale=sign)

        def phi(dst, raw, ex):
            nc.vector.scalar_tensor_tensor(out=dst, in0=raw, scalar=1.0, in1=ex, op0=ALU.add, op1=ALU.max)

        def quant(pair, src):
            nc.vector.quantize_mx(out=pair[0][:].bitcast(FP8X4), scales=pair[1][:], in_=src[:])

        def k_mul(h):
            nc.vector.tensor_tensor(
                out=fk[h // 2][:].rearrange("p (x g a j) -> p g a j x", x=PACK, g=2, j=PACK)[:, h % 2],
                in0=k_phi[h][:].rearrange("p (j a x) -> p a j x", j=PACK, x=PACK),
                in1=tk[:].rearrange("p (j a x) -> p a j x", j=PACK, x=PACK),
                op=ALU.mult,
            )

        def v_round(h):
            nc.scalar.copy(
                out=vb[h // 2][:, (h % 2) * 512 : (h % 2 + 1) * 512].rearrange("p (c i j) -> p c j i", i=2, j=PACK),
                in_=v_raw[h][:].rearrange("p (j c i) -> p c j i", j=PACK, i=2),
            )

        def jn(ap):
            return ap.rearrange("p (j n) -> p j n", j=PACK)

        q_src = [jn(q_raw[c // 2][:])[:, :, (c % 2) * P : (c % 2 + 1) * P] for c in range(4)]

        def q_neg_s(c):
            neg_s(jn(q_neg[c][:]), q_src[c])

        def q_exp_s(c):
            exp_s(q_exp[c][:], q_neg[c][:], -1.0)

        def q_phi(c):
            phi(jn(q_map[c][:]), q_src[c], jn(q_exp[c][:]))

        def q_mul_a(c):
            nc.vector.tensor_tensor(
                out=fq_a[:].rearrange("p (r s j) -> p s j r", r=2, j=PACK)[:, 64 * c : 64 * (c + 1)],
                in0=q_map[c][:].rearrange("p (j s r) -> p s j r", j=PACK, r=2),
                in1=qa_sb[:, 0:PACK].unsqueeze(1).unsqueeze(3).to_broadcast([P, 64, PACK, 2]),
                op=ALU.mult,
            )

        def q_mul_b(c):
            nc.vector.tensor_tensor(
                out=fq_b[c][:].rearrange("p (c i j) -> p c j i", i=2, j=PACK),
                in0=q_map[2 + c][:].rearrange("p (j c i) -> p c j i", j=PACK, i=2),
                in1=qa_sb[:, 0:PACK].unsqueeze(1).unsqueeze(3).to_broadcast([P, 64, PACK, 2]),
                op=ALU.mult,
            )

        def read_state(bank_ap, h, pair, cols):
            rows = slice(ROWS * h, ROWS * (h + 1))
            nc.tensor.matmul_mx(
                out=bank_ap,
                lhsT=pair[0][rows, cols].bitcast(FP8X4),
                lhsT_scale=pair[1][rows, cols],
                rhs=s_mx[0][rows, :].bitcast(FP8X4),
                rhs_scale=s_mx[1][rows, :],
                start=True,
                stop=True,
            )

        def k_quant(a):
            nc.vector.quantize_mx(
                out=k_codes[a][:].bitcast(FP8X4), scales=k_scales[:, 384 * a + 64 : 384 * a + 320], in_=fk[a][:]
            )

        def k_spread(a):
            live = k_wide[a][:, :, 64 * a : 64 * a + 2 * STRIDE].rearrange("p x (g c) -> p x g c", c=STRIDE)
            nc.vector.tensor_copy(
                out=live[:, :, :, 0:ROWS],
                in_=k_codes[a][:].rearrange("p (x g c) -> p x g c", x=PACK, g=2),
            )

        def build_state(a):
            for x in range(PACK):
                first = 384 * a + 64 * x + 64 * (1 - a)
                for g in range(2):
                    cols = slice(g * E, (g + 1) * E)
                    nc.tensor.matmul_mx(
                        out=s_bank[:, x, :],
                        lhsT=k_wide[a][:, x, P * g : P * (g + 1)].bitcast(FP8X4),
                        lhsT_scale=k_scales[:, first : first + P],
                        rhs=v_mx[a][0][:, cols].bitcast(FP8X4),
                        rhs_scale=v_mx[a][1][:, cols],
                        start=(a == 0 and x == 0 and g == 0),
                        stop=(a == 1 and x == PACK - 1 and g == 1),
                    )

        def state_out():
            nc.scalar.activation(
                out=s_bf[:].rearrange("p (e x) -> p e x", x=PACK),
                in_=s_bank[:].rearrange("p x e -> p e x"),
                func=ACT.Copy,
                scale=1.0 / N,
            )

        nc.vector.memset(k_scales[:].bitcast(I32), 0)
        for a in range(2):
            nc.vector.memset(k_wide[a][:, :, 0 : 2 * P], 0)
        for u in range(2):
            half = slice(u * 256, (u + 1) * 256)
            neg_v(k_neg[0][:, half], k0_half[u][:])
            exp_s(k_exp[0][:, half], k_neg[0][:, half], 1.0)
        for j in range(PACK):
            nc.vector.tensor_scalar(
                out=tk[:, j * D : (j + 1) * D], in0=ka_sb[:], scalar1=t_sb[:, j : j + 1], scalar2=None, op0=ALU.mult
            )
        neg_v(k_neg[1][:], k_raw[1][:])
        exp_s(k_exp[1][:], k_neg[1][:], 1.0)
        for u in range(2):
            half = slice(u * 256, (u + 1) * 256)
            phi(k_phi[0][:, half], k0_half[u][:], k_exp[0][:, half])
        neg_v(k_neg[2][:], k_raw[2][:])
        exp_s(k_exp[2][:], k_neg[2][:], 1.0)
        neg_s(k_neg[3][:], k_raw[3][:])
        v_round(0)
        exp_s(k_exp[3][:], k_neg[3][:], -1.0)
        for h in range(1, H):
            v_round(h)
        k_mul(0)
        phi(k_phi[1][:], k_raw[1][:], k_exp[1][:])
        phi(k_phi[2][:], k_raw[2][:], k_exp[2][:])
        k_mul(1)
        k_mul(2)
        k_quant(0)
        phi(k_phi[3][:], k_raw[3][:], k_exp[3][:])
        k_spread(0)
        quant(v_mx[0], vb[0])
        k_mul(3)
        build_state(0)
        neg_v(jn(q_neg[1][:]), q_src[1])
        k_quant(1)
        quant(v_mx[1], vb[1])
        k_spread(1)
        build_state(1)

        q_neg_s(0)
        q_exp_s(0)
        exp_s(q_exp[1][:], q_neg[1][:], 1.0)
        q_neg_s(2)
        q_neg_s(3)
        q_exp_s(2)
        state_out()
        q_exp_s(3)
        q_phi(0)
        q_phi(1)
        q_mul_a(0)
        q_mul_a(1)
        q_phi(2)
        quant(s_mx, s_bf)
        quant(qa_mx, fq_a)
        for h in range(H):
            for r in range(2):
                read_state(y_bank[h][:, r, :], h, qa_mx, slice(r * P, (r + 1) * P))
        out_a = out[:, 0:HALF, :].rearrange("h (s r) e -> s h (r e)", r=2)
        for h in range(H):
            nc.scalar.copy(out=y_a[h][:], in_=y_bank[h][:, 0:2, :].rearrange("p r e -> p (r e)"))
            nc.sync.dma_start(out=out_a[:, h, :], in_=y_a[h][:])
        q_mul_b(0)
        q_phi(3)
        quant(qb_mx[0], fq_b[0])
        q_mul_b(1)
        quant(qb_mx[1], fq_b[1])
        for c in range(2):
            banks = y_mid if c == 0 else y_bank
            for h in range(H):
                read_state(banks[h][:, 2 + c, :], h, qb_mx[c], slice(0, P))
            n0 = HALF + c * P
            out_b = out[:, n0 : n0 + P, :].rearrange("h s e -> s h e")
            y_view = y_b[c][:].rearrange("p (h e) -> p h e", h=H)
            for a in range(2):
                for h in (2 * a, 2 * a + 1):
                    if c == 1 and a == 1:
                        nc.vector.tensor_copy(out=y_view[:, h, :], in_=banks[h][:, 2 + c, :])
                    else:
                        nc.scalar.copy(out=y_view[:, h, :], in_=banks[h][:, 2 + c, :])
                queue = nc.scalar if (c == 1 and a == 0) else nc.sync
                queue.dma_start(out=out_b[:, 2 * a : 2 * a + 2, :], in_=y_view[:, 2 * a : 2 * a + 2, :])
